import numpy as np
import ml_dtypes


def mxq(x, axis, fmt="e4m3"):
    dtype, down = {"e4m3": (ml_dtypes.float8_e4m3fn, 7), "e5m2": (ml_dtypes.float8_e5m2, 14)}[fmt]
    v = np.moveaxis(np.asarray(x, np.float32).astype(ml_dtypes.bfloat16).astype(np.float64), axis, -1)
    blocks = v.reshape(v.shape[:-1] + (-1, 32))
    amax = np.abs(blocks).max(-1, keepdims=True)
    byte = np.maximum(np.where(amax > 0, np.frexp(amax)[1] - 1 + 127, 0) - down, 1)
    scale = np.exp2(byte - 127.0)
    codes = (blocks / scale).astype(np.float32).astype(dtype).astype(np.float64)
    return np.moveaxis((codes * scale).reshape(v.shape), -1, axis)


WIDE = False


def mx_kscale(k):
    if not WIDE:
        return np.ones(k)
    levels = np.array([10, -10, 5, -5, 0])
    if k % 512:
        return np.exp2(np.random.permutation(np.resize(levels, k // 32))).repeat(32)
    a = np.empty((k // 512, 16))
    for p in range(k // 512):
        a[p, :8] = np.random.permutation(np.resize(levels, 8))
        for g in range(8):
            far = levels[np.abs(levels - a[p, g]) >= 10]
            a[p, g + 8] = far[np.random.randint(len(far))]
    return np.exp2(a.ravel()).repeat(32)


def f64(x):
    return np.asarray(x).astype(np.float64)


def striped(idx):
    return np.tile(np.asarray(idx).reshape(-1, 16).T, (8, 1)).astype(np.uint16)


def unstriped(offs):
    return offs[:16].T.reshape(-1).astype(np.int64)


def striped8(idx):
    return np.asarray(idx).reshape(8, -1, 16).transpose(0, 2, 1).reshape(128, -1).astype(np.uint16)


def unstriped8(offs):
    return offs.reshape(8, 16, -1).transpose(0, 2, 1).reshape(8, -1).astype(np.int64)


def pick8(x, idx, run):
    r = np.arange(len(x))
    return x[r[:, None], idx[r % (8 * run) // run]]


E2M1 = np.array([0.0, 0.5, 1.0, 1.5, 2.0, 3.0, 4.0, 6.0, -0.0, -0.5, -1.0, -1.5, -2.0, -3.0, -4.0, -6.0])


def pack_weight(w, fmt):
    k, n = w.shape
    w = f64(np.asarray(w, np.float32).astype(ml_dtypes.bfloat16)).reshape(k // 32, 32, n)
    amax = np.abs(w).max(1)
    if fmt == "e4m3":
        byte = np.frexp(amax)[1] - 1 + 127 - 7
    else:
        mant, ex = np.frexp(amax / 6.0)
        byte = np.where(mant > 0.5, ex, ex - 1) + 127
    byte = np.clip(np.where(amax > 0, byte, 1), 1, 254)
    scaled = (w * np.exp2(127.0 - byte)[:, None, :]).reshape(k, n).astype(np.float32)
    by_word = np.ascontiguousarray(scaled.reshape(k // 512, 128, 4, n).transpose(0, 1, 3, 2))
    if fmt == "e4m3":
        words = by_word.astype(ml_dtypes.float8_e4m3fn).view(np.uint8)
    else:
        c = by_word.astype(ml_dtypes.float4_e2m1fn).view(np.uint8) & 0xF
        words = (c[..., 0::2] | (c[..., 1::2] << 4)).reshape(k // 512, 128, 2 * n)
    return np.ascontiguousarray(words), np.ascontiguousarray(byte.astype(np.uint8).reshape(k // 512, 16, n))


def unpack_weight(words, scales, fmt):
    g, _, n = scales.shape
    words = np.ascontiguousarray(words).reshape(g, 128, n, -1)
    if fmt == "e4m3":
        vals = words.view(ml_dtypes.float8_e4m3fn).astype(np.float64)
    else:
        nib = np.empty((g, 128, n, 4), np.uint8)
        nib[..., 0::2] = words & 0xF
        nib[..., 1::2] = words >> 4
        vals = E2M1[nib]
    vals = vals * np.repeat(np.exp2(scales.astype(np.float64) - 127.0), 8, axis=1)[..., None]
    return vals.transpose(0, 1, 3, 2).reshape(g * 512, n)


def sgn(shape):
    return np.random.uniform(0.5, 2.0, shape) * np.where(np.random.standard_normal(shape) < 0, -1.0, 1.0)


K, J, R, T, F, O, N, S, U, E = 512, 512, 512, 1024, 1024, 256, 256, 512, 128, 512


def setup_inputs():
    n = np.random.standard_normal
    idx = np.stack([np.random.permutation(T)[:J] for _ in range(8)])
    idx2 = np.random.permutation(F)[:R]
    idx3 = np.stack([np.random.permutation(J)[:O] for _ in range(8)])
    idx4 = np.stack([np.random.permutation(J)[:O] for _ in range(8)])
    idx5 = np.stack([np.random.permutation(S)[:N] for _ in range(8)])
    idx6 = np.stack([np.random.permutation(O)[:U] for _ in range(8)])
    idx7 = np.stack([np.random.permutation(E)[:U] for _ in range(8)])
    fk = mx_kscale(K)
    fr = mx_kscale(R)
    tr = np.ones(F)
    tr[idx2] = fr
    wtp = pack_weight(n((K, F)) * 1 / np.sqrt(K) / fk[:, None] * tr, "e2m1")
    return {
        "ta": (np.random.randint(-7, 8, (K, T)).astype(np.float64)).astype(np.float32),
        "ga": ((np.random.randint(8, 25, (K, 1)) / 64.0) * fk[:, None]).astype(np.float32),
        "wt_words": wtp[0],
        "wt_scales": wtp[1],
        "sa": (np.random.uniform(0.5, 1.6, (R, 1))).astype(np.float32),
        "sb": (np.random.uniform(0.5, 1.6, (R, 1))).astype(np.float32),
        "va": (np.random.randint(-7, 8, (R, S)).astype(np.float64)).astype(np.float32),
        "ea": ((np.random.randint(8, 25, (R, 1)) / 1024.0) / fr[:, None]).astype(np.float32),
        "so": (sgn((N, 1))).astype(np.float32),
        "offs": striped8(idx),
        "offs2": striped(idx2),
        "offs3": striped8(idx3),
        "offs4": striped8(idx4),
        "offs5": striped8(idx5),
        "offs6": striped8(idx6),
        "offs7": striped8(idx7),
    }


def reference(ta, ga, wt_words, wt_scales, sa, sb, va, ea, so, offs, offs2, offs3, offs4, offs5, offs6, offs7):
    idx = unstriped8(offs)
    idx2 = unstriped(offs2)
    idx3 = unstriped8(offs3)
    idx4 = unstriped8(offs4)
    idx5 = unstriped8(offs5)
    idx6 = unstriped8(offs6)
    idx7 = unstriped8(offs7)
    wtu = unpack_weight(wt_words, wt_scales, "e2m1")
    xc = pick8(f64(ta), idx, 64) * f64(ga)
    wtidx2g = wtu[:, idx2]
    xcq = mxq(xc, 0, "e4m3")
    a = wtidx2g.T @ xcq
    hid = np.maximum(pick8(a, idx3, 64) * f64(sa), pick8(a, idx4, 64) * f64(sb))
    vc = pick8(f64(va), idx5, 64) * f64(ea)
    vcq = mxq(vc, 0, "e4m3")
    hidq = mxq(hid, 0, "e4m3")
    p = vcq.T @ hidq
    m0 = pick8(p, idx6, 16) * f64(so)
    y = np.zeros((N, E))
    y[np.arange(N)[:, None], idx7[np.arange(N) % 128 // 16]] = m0
    return y

@@ -1,0 +1,214 @@
+from contextlib import ExitStack
+
+import concourse.mybir as mybir
+
+F32 = mybir.dt.float32
+BF16 = mybir.dt.bfloat16
+I32 = mybir.dt.int32
+U32 = mybir.dt.uint32
+U16 = mybir.dt.uint16
+U8 = mybir.dt.uint8
+FP8X4 = mybir.dt.float8_e4m3fn_x4
+FP4X4 = mybir.dt.float4_e2m1fn_x4
+COPY = mybir.ActivationFunctionType.Copy
+MAX = mybir.AluOpType.max
+
+K, J, R, T, F, O, N, S, U, E = 512, 512, 512, 1024, 1024, 256, 256, 512, 128, 512
+P = 128
+PACK = 4
+FLOPS = 2 * K * R * J + 2 * R * N * O
+
+
+def tile_picked_codes_store_one_grouppair_codes_posted_kernel(
+    tc, ta, ga, wt_words, wt_scales, sa, sb, va, ea, so, offs, offs2, offs3, offs4, offs5, offs6, offs7, out
+):
+    nc = tc.nc
+    with ExitStack() as ctx:
+        sb_pool = ctx.enter_context(tc.tile_pool(name="held", bufs=1))
+        psum = ctx.enter_context(tc.psum_pool(name="psum", bufs=1))
+
+        def tile(name, shape, dtype):
+            return sb_pool.tile(shape, dtype, name=name, align_bytes=64)
+
+        def load_list(name, src):
+            lst = tile(name, list(src.shape), U16)
+            nc.sync.dma_start(lst[:], src)
+            return lst
+
+        def load_plane(name, src, t):
+            plane = tile(name, [P, src.shape[1]], F32)
+            nc.sync.dma_start(plane[:], src.rearrange("(p t) c -> t p c", t=PACK)[t])
+            return plane
+
+        def load_factor(queue, name, src):
+            fac = tile(name, [P, PACK], F32)
+            queue.dma_start(fac[:], src.rearrange("(p t) o -> p (t o)", t=PACK))
+            return fac
+
+        def entries(lst, first, count):
+            return lst[:, first // 16 : (first + count) // 16]
+
+        scale_rows = tile("scale_rows", [PACK, 4, F // 4], I32)
+        nc.scalar.dma_start(scale_rows[:], wt_scales[0].bitcast(I32).rearrange("(q i) c -> i q c", i=4))
+        ga_t = load_factor(nc.scalar, "ga_t", ga)
+        ta_p = [load_plane("ta0", ta, 0)]
+        l1 = load_list("l1", offs)
+        l2 = load_list("l2", offs2)
+        ta_p.append(load_plane("ta1", ta, 1))
+        w_win = tile("w_win", [P, F], U16)
+        nc.sync.dma_start(w_win[:].bitcast(I32), wt_words[0].bitcast(I32))
+        for t in range(2, PACK):
+            ta_p.append(load_plane("ta%d" % t, ta, t))
+        l5 = load_list("l5", offs5)
+        ea_t = load_factor(nc.sync, "ea_t", ea)
+        va_p = [load_plane("va%d" % t, va, t) for t in range(PACK)]
+        l3 = load_list("l3", offs3)
+        sa_t = load_factor(nc.sync, "sa_t", sa)
+        l4 = load_list("l4", offs4)
+        sb_t = load_factor(nc.sync, "sb_t", sb)
+        l6 = load_list("l6", offs6)
+        so_t = tile("so_t", [P, 2], F32)
+        with nc.allow_non_contiguous_dma(reason="one value a partition"):
+            nc.sync.dma_start(so_t[:], so.rearrange("(i p) o -> p (i o)", p=P))
+        l7 = load_list("l7", offs7)
+
+        s_win = tile("s_win", [P, F], U8)
+        nc.vector.memset(s_win[:].bitcast(I32), 0)
+        pages = [tile("page%d" % i, [P, E], F32) for i in range(2)]
+        for page in pages:
+            nc.vector.memset(page[:], 0.0)
+        for q in range(4):
+            nc.vector.tensor_copy(s_win[32 * q : 32 * q + 4, :].bitcast(I32), scale_rows[:, q, :])
+        w_scales = tile("w_scales", [P, R], U8)
+        nc.vector.tensor_copy(w_scales[:].rearrange("p (t m) -> p m t", t=PACK), s_win[:].indirect(l2[:]))
+        w_listed = tile("w_listed", [P, R], U16)
+        nc.vector.tensor_copy(w_listed[:], w_win[:].indirect(l2[:]))
+        w_dealt = tile("w_dealt", [P, R], U16)
+        nc.vector.tensor_copy(
+            w_dealt[:].rearrange("p (t m) -> p t m", t=PACK), w_listed[:].rearrange("p (m t) -> p t m", t=PACK)
+        )
+
+        half_j = J // 2
+        xc_low = tile("xc_low", [P, 2, J], BF16)
+        xc_high = [tile("xc_high%d" % h, [P, 2, half_j], BF16) for h in range(2)]
+        xc_woven = [tile("xc_woven%d" % h, [P, half_j, PACK], BF16) for h in range(2)]
+        for t in range(2):
+            nc.scalar.activation(xc_low[:, t, :], ta_p[t][:].indirect(l1[:]), COPY, scale=ga_t[:, t : t + 1])
+        for h in range(2):
+            nc.vector.tensor_copy(
+                xc_woven[h][:, :, 0:2], xc_low[:, :, h * half_j : (h + 1) * half_j].rearrange("p t j -> p j t")
+            )
+        for t in range(2, PACK):
+            for h in range(2):
+                nc.scalar.activation(
+                    xc_high[h][:, t - 2, :],
+                    ta_p[t][:].indirect(entries(l1, h * half_j, half_j)),
+                    COPY,
+                    scale=ga_t[:, t : t + 1],
+                )
+        x_codes = tile("x_codes", [P, J], U32)
+        x_scales = tile("x_scales", [P, J], U8)
+        for h in range(2):
+            nc.vector.tensor_copy(xc_woven[h][:, :, 2:4], xc_high[h][:].rearrange("p t j -> p j t"))
+        for h in range(2):
+            cols = slice(h * half_j, (h + 1) * half_j)
+            nc.vector.quantize_mx(
+                x_codes[:, cols].bitcast(FP8X4), x_scales[:, cols], xc_woven[h][:].rearrange("p j t -> p (j t)")
+            )
+
+        vc = tile("vc", [P, PACK, N], BF16)
+        for t in range(PACK):
+            nc.scalar.activation(vc[:, t, :], va_p[t][:].indirect(l5[:]), COPY, scale=ea_t[:, t : t + 1])
+
+        def first_product(bank, t, cols):
+            nc.tensor.matmul_mx(
+                bank,
+                lhsT=w_dealt[:, t * P : (t + 1) * P].bitcast(U8).bitcast(FP4X4),
+                lhsT_scale=w_scales[:, t * P : (t + 1) * P],
+                rhs=x_codes[:, cols].bitcast(FP8X4),
+                rhs_scale=x_scales[:, cols],
+                start=True,
+                stop=True,
+            )
+
+        a_rows = [tile("a%d" % t, [P, J], F32) for t in range(PACK)]
+        for h in range(2):
+            cols = slice(h * half_j, (h + 1) * half_j)
+            bank = psum.tile([P, half_j], F32, name="a0_bank%d" % h)
+            first_product(bank[:], 0, cols)
+            nc.vector.tensor_copy(a_rows[0][:, cols], bank[:])
+        for t in range(1, PACK):
+            bank = psum.tile([P, J], F32, name="a_bank%d" % t)
+            first_product(bank[:], t, slice(0, J))
+            nc.vector.tensor_copy(a_rows[t][:], bank[:])
+
+        vc_woven = tile("vc_woven", [P, N, PACK], BF16)
+        nc.vector.tensor_copy(vc_woven[:], vc[:].rearrange("p t n -> p n t"))
+        v_codes = tile("v_codes", [P, N], U32)
+        v_scales = tile("v_scales", [P, N], U8)
+        nc.vector.quantize_mx(v_codes[:].bitcast(FP8X4), v_scales[:], vc_woven[:].rearrange("p n t -> p (n t)"))
+
+        half_o = O // 2
+        sides = ((l3, sa_t), (l4, sb_t))
+        low = [tile("low%d" % s, [P, 2, O], F32) for s in range(2)]
+        high = [[tile("high%d_%d" % (h, s), [P, 2, half_o], F32) for s in range(2)] for h in range(2)]
+        hid_woven = [tile("hid_woven%d" % h, [P, half_o, PACK], BF16) for h in range(2)]
+        for t in range(2):
+            for s, (lst, fac) in enumerate(sides):
+                nc.scalar.activation(low[s][:, t, :], a_rows[t][:].indirect(lst[:]), COPY, scale=fac[:, t : t + 1])
+        for h in range(2):
+            cols = slice(h * half_o, (h + 1) * half_o)
+            nc.vector.tensor_tensor(
+                hid_woven[h][:, :, 0:2],
+                low[0][:, :, cols].rearrange("p t o -> p o t"),
+                low[1][:, :, cols].rearrange("p t o -> p o t"),
+                MAX,
+            )
+        h_codes = tile("h_codes", [P, O], U32)
+        h_scales = tile("h_scales", [P, O], U8)
+        p_rows = [tile("p%d" % i, [P, O], F32) for i in range(2)]
+        for h in range(2):
+            cols = slice(h * half_o, (h + 1) * half_o)
+            for t in range(2, PACK):
+                for s, (lst, fac) in enumerate(sides):
+                    nc.scalar.activation(
+                        high[h][s][:, t - 2, :],
+                        a_rows[t][:].indirect(entries(lst, h * half_o, half_o)),
+                        COPY,
+                        scale=fac[:, t : t + 1],
+                    )
+            nc.vector.tensor_tensor(
+                hid_woven[h][:, :, 2:4],
+                high[h][0][:].rearrange("p t o -> p o t"),
+                high[h][1][:].rearrange("p t o -> p o t"),
+                MAX,
+            )
+            nc.vector.quantize_mx(
+                h_codes[:, cols].bitcast(FP8X4), h_scales[:, cols], hid_woven[h][:].rearrange("p o t -> p (o t)")
+            )
+            if h == 0:
+                shared = psum.tile([P, 2, half_o], F32, name="p_first")
+                banks = [shared[:, i, :] for i in range(2)]
+            else:
+                banks = [psum.tile([P, half_o], F32, name="p_last%d" % i)[:] for i in range(2)]
+            for i in range(2):
+                nc.tensor.matmul_mx(
+                    banks[i],
+                    lhsT=v_codes[:, i * P : (i + 1) * P].bitcast(FP8X4),
+                    lhsT_scale=v_scales[:, i * P : (i + 1) * P],
+                    rhs=h_codes[:, cols].bitcast(FP8X4),
+                    rhs_scale=h_scales[:, cols],
+                    start=True,
+                    stop=True,
+                )
+            for i in range(2):
+                if h == 1 and i == 0:
+                    nc.scalar.copy(p_rows[i][:, cols], banks[i])
+                else:
+                    nc.vector.tensor_copy(p_rows[i][:, cols], banks[i])
+
+        for i in range(2):
+            ends = tile("ends%d" % i, [P, U], F32)
+            nc.scalar.activation(ends[:], p_rows[i][:].indirect(l6[:]), COPY, scale=so_t[:, i : i + 1])
+            nc.vector.tensor_copy(pages[i][:].indirect(l7[:]), ends[:])
+            nc.sync.dma_start(out[i * P : (i + 1) * P, :], pages[i][:])

@@ -72,6 +72,11 @@ def tile_picked_codes_store_one_grouppair_codes_posted_kernel(
             nc.sync.dma_start(so_t[:], so.rearrange("(i p) o -> p (i o)", p=P))
         l7 = load_list("l7", offs7)
 
+        warm_in = tile("warm_in", [P, 1], F32)
+        warm_out = tile("warm_out", [P, 1], F32)
+        nc.vector.memset(warm_in[:], 0.0)
+        nc.scalar.activation(warm_out[:], warm_in[:], COPY)
+
         s_win = tile("s_win", [P, F], U8)
         nc.vector.memset(s_win[:].bitcast(I32), 0)
         pages = [tile("page%d" % i, [P, E], F32) for i in range(2)]

@@ -27,8 +27,8 @@ def tile_picked_codes_store_one_grouppair_codes_posted_kernel(
         sb_pool = ctx.enter_context(tc.tile_pool(name="held", bufs=1))
         psum = ctx.enter_context(tc.psum_pool(name="psum", bufs=1))
 
-        def tile(name, shape, dtype):
-            return sb_pool.tile(shape, dtype, name=name, align_bytes=64)
+        def tile(name, shape, dtype, tag=None):
+            return sb_pool.tile(shape, dtype, name=name, tag=tag or name, align_bytes=64)
 
         def load_list(name, src):
             lst = tile(name, list(src.shape), U16)
@@ -49,7 +49,7 @@ def tile_picked_codes_store_one_grouppair_codes_posted_kernel(
             return lst[:, first // 16 : (first + count) // 16]
 
         scale_rows = tile("scale_rows", [PACK, 4, F // 4], I32)
-        nc.scalar.dma_start(scale_rows[:], wt_scales[0].bitcast(I32).rearrange("(q i) c -> i q c", i=4))
+        nc.sync.dma_start(scale_rows[:], wt_scales[0].bitcast(I32).rearrange("(q i) c -> i q c", i=4))
         ga_t = load_factor(nc.scalar, "ga_t", ga)
         ta_p = [load_plane("ta0", ta, 0)]
         l1 = load_list("l1", offs)
@@ -95,7 +95,7 @@ def tile_picked_codes_store_one_grouppair_codes_posted_kernel(
 
         half_j = J // 2
         xc_low = tile("xc_low", [P, 2, J], BF16)
-        xc_high = [tile("xc_high%d" % h, [P, 2, half_j], BF16) for h in range(2)]
+        xc_high = tile("xc_high", [P, 2, J], BF16)
         xc_woven = [tile("xc_woven%d" % h, [P, half_j, PACK], BF16) for h in range(2)]
         for t in range(2):
             nc.scalar.activation(xc_low[:, t, :], ta_p[t][:].indirect(l1[:]), COPY, scale=ga_t[:, t : t + 1])
@@ -103,18 +103,18 @@ def tile_picked_codes_store_one_grouppair_codes_posted_kernel(
             nc.vector.tensor_copy(
                 xc_woven[h][:, :, 0:2], xc_low[:, :, h * half_j : (h + 1) * half_j].rearrange("p t j -> p j t")
             )
-        for t in range(2, PACK):
-            for h in range(2):
-                nc.scalar.activation(
-                    xc_high[h][:, t - 2, :],
-                    ta_p[t][:].indirect(entries(l1, h * half_j, half_j)),
-                    COPY,
-                    scale=ga_t[:, t : t + 1],
-                )
+        nc.scalar.activation(xc_high[:, 0, :], ta_p[2][:].indirect(l1[:]), COPY, scale=ga_t[:, 2:3])
+        for h in range(2):
+            nc.scalar.activation(
+                xc_high[:, 1, h * half_j : (h + 1) * half_j],
+                ta_p[3][:].indirect(entries(l1, h * half_j, half_j)),
+                COPY,
+                scale=ga_t[:, 3:4],
+            )
         x_codes = tile("x_codes", [P, J], U32)
         x_scales = tile("x_scales", [P, J], U8)
         for h in range(2):
-            nc.vector.tensor_copy(xc_woven[h][:, :, 2:4], xc_high[h][:].rearrange("p t j -> p j t"))
+            nc.vector.tensor_copy(xc_woven[h][:, :, 2:4], xc_high[:, :, h * half_j : (h + 1) * half_j].rearrange("p t j -> p j t"))
         for h in range(2):
             cols = slice(h * half_j, (h + 1) * half_j)
             nc.vector.quantize_mx(
@@ -156,7 +156,6 @@ def tile_picked_codes_store_one_grouppair_codes_posted_kernel(
         half_o = O // 2
         sides = ((l3, sa_t), (l4, sb_t))
         low = [tile("low%d" % s, [P, 2, O], F32) for s in range(2)]
-        high = [[tile("high%d_%d" % (h, s), [P, 2, half_o], F32) for s in range(2)] for h in range(2)]
         hid_woven = [tile("hid_woven%d" % h, [P, half_o, PACK], BF16) for h in range(2)]
         for t in range(2):
             for s, (lst, fac) in enumerate(sides):
@@ -169,23 +168,25 @@ def tile_picked_codes_store_one_grouppair_codes_posted_kernel(
                 low[1][:, :, cols].rearrange("p t o -> p o t"),
                 MAX,
             )
+        high = [tile("high%d" % s, [P, 2, O], F32, tag="a%d" % s) for s in range(2)]
+        for s, (lst, fac) in enumerate(sides):
+            nc.scalar.activation(high[s][:, 0, :], a_rows[2][:].indirect(lst[:]), COPY, scale=fac[:, 2:3])
         h_codes = tile("h_codes", [P, O], U32)
         h_scales = tile("h_scales", [P, O], U8)
         p_rows = [tile("p%d" % i, [P, O], F32) for i in range(2)]
         for h in range(2):
             cols = slice(h * half_o, (h + 1) * half_o)
-            for t in range(2, PACK):
-                for s, (lst, fac) in enumerate(sides):
-                    nc.scalar.activation(
-                        high[h][s][:, t - 2, :],
-                        a_rows[t][:].indirect(entries(lst, h * half_o, half_o)),
-                        COPY,
-                        scale=fac[:, t : t + 1],
-                    )
+            for s, (lst, fac) in enumerate(sides):
+                nc.scalar.activation(
+                    high[s][:, 1, cols],
+                    a_rows[3][:].indirect(entries(lst, h * half_o, half_o)),
+                    COPY,
+                    scale=fac[:, 3:4],
+                )
             nc.vector.tensor_tensor(
                 hid_woven[h][:, :, 2:4],
-                high[h][0][:].rearrange("p t o -> p o t"),
-                high[h][1][:].rearrange("p t o -> p o t"),
+                high[0][:, :, cols].rearrange("p t o -> p o t"),
+                high[1][:, :, cols].rearrange("p t o -> p o t"),
                 MAX,
             )
             nc.vector.quantize_mx(

@@ -54,10 +54,9 @@ def tile_picked_codes_store_one_grouppair_codes_posted_kernel(
         ta_p = [load_plane("ta0", ta, 0)]
         l1 = load_list("l1", offs)
         l2 = load_list("l2", offs2)
-        ta_p.append(load_plane("ta1", ta, 1))
         w_win = tile("w_win", [P, F], U16)
         nc.sync.dma_start(w_win[:].bitcast(I32), wt_words[0].bitcast(I32))
-        for t in range(2, PACK):
+        for t in range(1, PACK):
             ta_p.append(load_plane("ta%d" % t, ta, t))
         l5 = load_list("l5", offs5)
         ea_t = load_factor(nc.sync, "ea_t", ea)
@@ -115,11 +114,11 @@ def tile_picked_codes_store_one_grouppair_codes_posted_kernel(
         x_scales = tile("x_scales", [P, J], U8)
         for h in range(2):
             nc.vector.tensor_copy(xc_woven[h][:, :, 2:4], xc_high[:, :, h * half_j : (h + 1) * half_j].rearrange("p t j -> p j t"))
-        for h in range(2):
-            cols = slice(h * half_j, (h + 1) * half_j)
-            nc.vector.quantize_mx(
-                x_codes[:, cols].bitcast(FP8X4), x_scales[:, cols], xc_woven[h][:].rearrange("p j t -> p (j t)")
-            )
+        pieces = (slice(0, half_j), slice(half_j, half_j + P), slice(half_j + P, J))
+        for cols in pieces:
+            h = cols.start // half_j
+            woven = xc_woven[h][:, cols.start - h * half_j : cols.stop - h * half_j, :]
+            nc.vector.quantize_mx(x_codes[:, cols].bitcast(FP8X4), x_scales[:, cols], woven.rearrange("p j t -> p (j t)"))
 
         vc = tile("vc", [P, PACK, N], BF16)
         for t in range(PACK):
@@ -137,9 +136,8 @@ def tile_picked_codes_store_one_grouppair_codes_posted_kernel(
             )
 
         a_rows = [tile("a%d" % t, [P, J], F32) for t in range(PACK)]
-        for h in range(2):
-            cols = slice(h * half_j, (h + 1) * half_j)
-            bank = psum.tile([P, half_j], F32, name="a0_bank%d" % h)
+        for h, cols in enumerate(pieces):
+            bank = psum.tile([P, cols.stop - cols.start], F32, name="a0_bank%d" % h)
             first_product(bank[:], 0, cols)
             nc.vector.tensor_copy(a_rows[0][:, cols], bank[:])
         for t in range(1, PACK):
@@ -192,26 +190,23 @@ def tile_picked_codes_store_one_grouppair_codes_posted_kernel(
             nc.vector.quantize_mx(
                 h_codes[:, cols].bitcast(FP8X4), h_scales[:, cols], hid_woven[h][:].rearrange("p o t -> p (o t)")
             )
-            if h == 0:
-                shared = psum.tile([P, 2, half_o], F32, name="p_first")
-                banks = [shared[:, i, :] for i in range(2)]
-            else:
-                banks = [psum.tile([P, half_o], F32, name="p_last%d" % i)[:] for i in range(2)]
-            for i in range(2):
-                nc.tensor.matmul_mx(
-                    banks[i],
-                    lhsT=v_codes[:, i * P : (i + 1) * P].bitcast(FP8X4),
-                    lhsT_scale=v_scales[:, i * P : (i + 1) * P],
-                    rhs=h_codes[:, cols].bitcast(FP8X4),
-                    rhs_scale=h_scales[:, cols],
-                    start=True,
-                    stop=True,
-                )
-            for i in range(2):
-                if h == 1 and i == 0:
-                    nc.scalar.copy(p_rows[i][:, cols], banks[i])
-                else:
-                    nc.vector.tensor_copy(p_rows[i][:, cols], banks[i])
+
+        def second_product(name, i, cols, engine_copy):
+            bank = psum.tile([P, cols.stop - cols.start], F32, name=name)
+            nc.tensor.matmul_mx(
+                bank[:],
+                lhsT=v_codes[:, i * P : (i + 1) * P].bitcast(FP8X4),
+                lhsT_scale=v_scales[:, i * P : (i + 1) * P],
+                rhs=h_codes[:, cols].bitcast(FP8X4),
+                rhs_scale=h_scales[:, cols],
+                start=True,
+                stop=True,
+            )
+            engine_copy(p_rows[i][:, cols], bank[:])
+
+        second_product("a0_bank0", 0, slice(0, half_o), nc.vector.tensor_copy)
+        second_product("p0_last", 0, slice(half_o, O), nc.scalar.copy)
+        second_product("p1", 1, slice(0, O), nc.vector.tensor_copy)
 
         for i in range(2):
             ends = tile("ends%d" % i, [P, U], F32)

from contextlib import ExitStack

import concourse.mybir as mybir

F32 = mybir.dt.float32
BF16 = mybir.dt.bfloat16
I32 = mybir.dt.int32
U32 = mybir.dt.uint32
U16 = mybir.dt.uint16
U8 = mybir.dt.uint8
FP8X4 = mybir.dt.float8_e4m3fn_x4
FP4X4 = mybir.dt.float4_e2m1fn_x4
COPY = mybir.ActivationFunctionType.Copy
MAX = mybir.AluOpType.max

K, J, R, T, F, O, N, S, U, E = 512, 512, 512, 1024, 1024, 256, 256, 512, 128, 512
P = 128
PACK = 4
FLOPS = 2 * K * R * J + 2 * R * N * O


def tile_picked_codes_store_one_grouppair_codes_posted_kernel(
    tc, ta, ga, wt_words, wt_scales, sa, sb, va, ea, so, offs, offs2, offs3, offs4, offs5, offs6, offs7, out
):
    nc = tc.nc
    with ExitStack() as ctx:
        sb_pool = ctx.enter_context(tc.tile_pool(name="held", bufs=1))
        psum = ctx.enter_context(tc.psum_pool(name="psum", bufs=1))

        def tile(name, shape, dtype, tag=None):
            return sb_pool.tile(shape, dtype, name=name, tag=tag or name, align_bytes=64)

        def load_list(name, src):
            lst = tile(name, list(src.shape), U16)
            nc.sync.dma_start(lst[:], src)
            return lst

        def load_plane(name, src, t):
            plane = tile(name, [P, src.shape[1]], F32)
            nc.sync.dma_start(plane[:], src.rearrange("(p t) c -> t p c", t=PACK)[t])
            return plane

        def load_factor(queue, name, src):
            fac = tile(name, [P, PACK], F32)
            queue.dma_start(fac[:], src.rearrange("(p t) o -> p (t o)", t=PACK))
            return fac

        def entries(lst, first, count):
            return lst[:, first // 16 : (first + count) // 16]

        scale_rows = tile("scale_rows", [PACK, 4, F // 4], I32)
        nc.sync.dma_start(scale_rows[:], wt_scales[0].bitcast(I32).rearrange("(q i) c -> i q c", i=4))
        ga_t = load_factor(nc.scalar, "ga_t", ga)
        ta_p = [load_plane("ta0", ta, 0)]
        l1 = load_list("l1", offs)
        l2 = load_list("l2", offs2)
        w_win = tile("w_win", [P, F], U16)
        nc.sync.dma_start(w_win[:].bitcast(I32), wt_words[0].bitcast(I32))
        for t in range(1, PACK):
            ta_p.append(load_plane("ta%d" % t, ta, t))
        l5 = load_list("l5", offs5)
        ea_t = load_factor(nc.sync, "ea_t", ea)
        va_p = [load_plane("va%d" % t, va, t) for t in range(PACK)]
        l3 = load_list("l3", offs3)
        sa_t = load_factor(nc.sync, "sa_t", sa)
        l4 = load_list("l4", offs4)
        sb_t = load_factor(nc.sync, "sb_t", sb)
        l6 = load_list("l6", offs6)
        so_t = tile("so_t", [P, 2], F32)
        with nc.allow_non_contiguous_dma(reason="one value a partition"):
            nc.sync.dma_start(so_t[:], so.rearrange("(i p) o -> p (i o)", p=P))
        l7 = load_list("l7", offs7)

        warm_in = tile("warm_in", [P, 1], F32)
        warm_out = tile("warm_out", [P, 1], F32)
        nc.vector.memset(warm_in[:], 0.0)
        nc.scalar.activation(warm_out[:], warm_in[:], COPY)

        s_win = tile("s_win", [P, F], U8)
        nc.vector.memset(s_win[:].bitcast(I32), 0)
        pages = [tile("page%d" % i, [P, E], F32) for i in range(2)]
        for page in pages:
            nc.vector.memset(page[:], 0.0)
        for q in range(4):
            nc.vector.tensor_copy(s_win[32 * q : 32 * q + 4, :].bitcast(I32), scale_rows[:, q, :])
        w_scales = tile("w_scales", [P, R], U8)
        nc.vector.tensor_copy(w_scales[:].rearrange("p (t m) -> p m t", t=PACK), s_win[:].indirect(l2[:]))
        w_listed = tile("w_listed", [P, R], U16)
        nc.vector.tensor_copy(w_listed[:], w_win[:].indirect(l2[:]))
        w_dealt = tile("w_dealt", [P, R], U16)
        nc.vector.tensor_copy(
            w_dealt[:].rearrange("p (t m) -> p t m", t=PACK), w_listed[:].rearrange("p (m t) -> p t m", t=PACK)
        )

        half_j = J // 2
        xc_low = tile("xc_low", [P, 2, J], BF16)
        xc_high = tile("xc_high", [P, 2, J], BF16)
        xc_woven = [tile("xc_woven%d" % h, [P, half_j, PACK], BF16) for h in range(2)]
        for t in range(2):
            nc.scalar.activation(xc_low[:, t, :], ta_p[t][:].indirect(l1[:]), COPY, scale=ga_t[:, t : t + 1])
        for h in range(2):
            nc.vector.tensor_copy(
                xc_woven[h][:, :, 0:2], xc_low[:, :, h * half_j : (h + 1) * half_j].rearrange("p t j -> p j t")
            )
        nc.scalar.activation(xc_high[:, 0, :], ta_p[2][:].indirect(l1[:]), COPY, scale=ga_t[:, 2:3])
        for h in range(2):
            nc.scalar.activation(
                xc_high[:, 1, h * half_j : (h + 1) * half_j],
                ta_p[3][:].indirect(entries(l1, h * half_j, half_j)),
                COPY,
                scale=ga_t[:, 3:4],
            )
        x_codes = tile("x_codes", [P, J], U32)
        x_scales = tile("x_scales", [P, J], U8)
        for h in range(2):
            nc.vector.tensor_copy(xc_woven[h][:, :, 2:4], xc_high[:, :, h * half_j : (h + 1) * half_j].rearrange("p t j -> p j t"))
        pieces = (slice(0, half_j), slice(half_j, half_j + P), slice(half_j + P, J))
        for cols in pieces:
            h = cols.start // half_j
            woven = xc_woven[h][:, cols.start - h * half_j : cols.stop - h * half_j, :]
            nc.vector.quantize_mx(x_codes[:, cols].bitcast(FP8X4), x_scales[:, cols], woven.rearrange("p j t -> p (j t)"))

        vc = tile("vc", [P, PACK, N], BF16)
        for t in range(PACK):
            nc.scalar.activation(vc[:, t, :], va_p[t][:].indirect(l5[:]), COPY, scale=ea_t[:, t : t + 1])

        def first_product(bank, t, cols):
            nc.tensor.matmul_mx(
                bank,
                lhsT=w_dealt[:, t * P : (t + 1) * P].bitcast(U8).bitcast(FP4X4),
                lhsT_scale=w_scales[:, t * P : (t + 1) * P],
                rhs=x_codes[:, cols].bitcast(FP8X4),
                rhs_scale=x_scales[:, cols],
                start=True,
                stop=True,
            )

        a_rows = [tile("a%d" % t, [P, J], F32) for t in range(PACK)]
        for h, cols in enumerate(pieces):
            bank = psum.tile([P, cols.stop - cols.start], F32, name="a0_bank%d" % h)
            first_product(bank[:], 0, cols)
            nc.vector.tensor_copy(a_rows[0][:, cols], bank[:])
        for t in range(1, PACK):
            bank = psum.tile([P, J], F32, name="a_bank%d" % t)
            first_product(bank[:], t, slice(0, J))
            nc.vector.tensor_copy(a_rows[t][:], bank[:])

        vc_woven = tile("vc_woven", [P, N, PACK], BF16)
        nc.vector.tensor_copy(vc_woven[:], vc[:].rearrange("p t n -> p n t"))
        v_codes = tile("v_codes", [P, N], U32)
        v_scales = tile("v_scales", [P, N], U8)
        nc.vector.quantize_mx(v_codes[:].bitcast(FP8X4), v_scales[:], vc_woven[:].rearrange("p n t -> p (n t)"))

        half_o = O // 2
        sides = ((l3, sa_t), (l4, sb_t))
        low = [tile("low%d" % s, [P, 2, O], F32) for s in range(2)]
        hid_woven = [tile("hid_woven%d" % h, [P, half_o, PACK], BF16) for h in range(2)]
        for t in range(2):
            for s, (lst, fac) in enumerate(sides):
                nc.scalar.activation(low[s][:, t, :], a_rows[t][:].indirect(lst[:]), COPY, scale=fac[:, t : t + 1])
        for h in range(2):
            cols = slice(h * half_o, (h + 1) * half_o)
            nc.vector.tensor_tensor(
                hid_woven[h][:, :, 0:2],
                low[0][:, :, cols].rearrange("p t o -> p o t"),
                low[1][:, :, cols].rearrange("p t o -> p o t"),
                MAX,
            )
        high = [tile("high%d" % s, [P, 2, O], F32, tag="a%d" % s) for s in range(2)]
        for s, (lst, fac) in enumerate(sides):
            nc.scalar.activation(high[s][:, 0, :], a_rows[2][:].indirect(lst[:]), COPY, scale=fac[:, 2:3])
        h_codes = tile("h_codes", [P, O], U32)
        h_scales = tile("h_scales", [P, O], U8)
        p_rows = [tile("p%d" % i, [P, O], F32) for i in range(2)]
        for h in range(2):
            cols = slice(h * half_o, (h + 1) * half_o)
            for s, (lst, fac) in enumerate(sides):
                nc.scalar.activation(
                    high[s][:, 1, cols],
                    a_rows[3][:].indirect(entries(lst, h * half_o, half_o)),
                    COPY,
                    scale=fac[:, 3:4],
                )
            nc.vector.tensor_tensor(
                hid_woven[h][:, :, 2:4],
                high[0][:, :, cols].rearrange("p t o -> p o t"),
                high[1][:, :, cols].rearrange("p t o -> p o t"),
                MAX,
            )
            nc.vector.quantize_mx(
                h_codes[:, cols].bitcast(FP8X4), h_scales[:, cols], hid_woven[h][:].rearrange("p o t -> p (o t)")
            )

        def second_product(name, i, cols, engine_copy):
            bank = psum.tile([P, cols.stop - cols.start], F32, name=name)
            nc.tensor.matmul_mx(
                bank[:],
                lhsT=v_codes[:, i * P : (i + 1) * P].bitcast(FP8X4),
                lhsT_scale=v_scales[:, i * P : (i + 1) * P],
                rhs=h_codes[:, cols].bitcast(FP8X4),
                rhs_scale=h_scales[:, cols],
                start=True,
                stop=True,
            )
            engine_copy(p_rows[i][:, cols], bank[:])

        second_product("a0_bank0", 0, slice(0, half_o), nc.vector.tensor_copy)
        second_product("p0_last", 0, slice(half_o, O), nc.scalar.copy)
        second_product("p1", 1, slice(0, O), nc.vector.tensor_copy)

        for i in range(2):
            ends = tile("ends%d" % i, [P, U], F32)
            nc.scalar.activation(ends[:], p_rows[i][:].indirect(l6[:]), COPY, scale=so_t[:, i : i + 1])
            nc.vector.tensor_copy(pages[i][:].indirect(l7[:]), ends[:])
            nc.sync.dma_start(out[i * P : (i + 1) * P, :], pages[i][:])
